import numpy as np
import ml_dtypes


def mxq(x, axis, fmt="e4m3"):
    dtype, down = {"e4m3": (ml_dtypes.float8_e4m3fn, 7), "e5m2": (ml_dtypes.float8_e5m2, 14)}[fmt]
    v = np.moveaxis(np.asarray(x, np.float32).astype(ml_dtypes.bfloat16).astype(np.float64), axis, -1)
    blocks = v.reshape(v.shape[:-1] + (-1, 32))
    amax = np.abs(blocks).max(-1, keepdims=True)
    byte = np.maximum(np.where(amax > 0, np.frexp(amax)[1] - 1 + 127, 0) - down, 1)
    scale = np.exp2(byte - 127.0)
    codes = (blocks / scale).astype(np.float32).astype(dtype).astype(np.float64)
    return np.moveaxis((codes * scale).reshape(v.shape), -1, axis)


WIDE = False


def mx_kscale(k):
    if not WIDE:
        return np.ones(k)
    levels = np.array([10, -10, 5, -5, 0])
    if k % 512:
        return np.exp2(np.random.permutation(np.resize(levels, k // 32))).repeat(32)
    a = np.empty((k // 512, 16))
    for p in range(k // 512):
        a[p, :8] = np.random.permutation(np.resize(levels, 8))
        for g in range(8):
            far = levels[np.abs(levels - a[p, g]) >= 10]
            a[p, g + 8] = far[np.random.randint(len(far))]
    return np.exp2(a.ravel()).repeat(32)


def f64(x):
    return np.asarray(x).astype(np.float64)


def striped(idx):
    return np.tile(idx.reshape(-1, 16).T, (8, 1)).astype(np.uint16)


def unstriped(offs):
    return offs[:16].T.reshape(-1).astype(np.int64)


E2M1 = np.array([0.0, 0.5, 1.0, 1.5, 2.0, 3.0, 4.0, 6.0, -0.0, -0.5, -1.0, -1.5, -2.0, -3.0, -4.0, -6.0])


def pack_weight(w, fmt):
    k, n = w.shape
    w = f64(np.asarray(w, np.float32).astype(ml_dtypes.bfloat16)).reshape(k // 32, 32, n)
    amax = np.abs(w).max(1)
    if fmt == "e4m3":
        byte = np.frexp(amax)[1] - 1 + 127 - 7
    else:
        mant, ex = np.frexp(amax / 6.0)
        byte = np.where(mant > 0.5, ex, ex - 1) + 127
    byte = np.clip(np.where(amax > 0, byte, 1), 1, 254)
    scaled = (w * np.exp2(127.0 - byte)[:, None, :]).reshape(k, n).astype(np.float32)
    by_word = np.ascontiguousarray(scaled.reshape(k // 512, 128, 4, n).transpose(0, 1, 3, 2))
    if fmt == "e4m3":
        words = by_word.astype(ml_dtypes.float8_e4m3fn).view(np.uint8)
    else:
        c = by_word.astype(ml_dtypes.float4_e2m1fn).view(np.uint8) & 0xF
        words = (c[..., 0::2] | (c[..., 1::2] << 4)).reshape(k // 512, 128, 2 * n)
    return np.ascontiguousarray(words), np.ascontiguousarray(byte.astype(np.uint8).reshape(k // 512, 16, n))


def unpack_weight(words, scales, fmt):
    g, _, n = scales.shape
    words = np.ascontiguousarray(words).reshape(g, 128, n, -1)
    if fmt == "e4m3":
        vals = words.view(ml_dtypes.float8_e4m3fn).astype(np.float64)
    else:
        nib = np.empty((g, 128, n, 4), np.uint8)
        nib[..., 0::2] = words & 0xF
        nib[..., 1::2] = words >> 4
        vals = E2M1[nib]
    vals = vals * np.repeat(np.exp2(scales.astype(np.float64) - 127.0), 8, axis=1)[..., None]
    return vals.transpose(0, 1, 3, 2).reshape(g * 512, n)


def gelu(v):
    return 0.5 * v * (1.0 + np.tanh(np.sqrt(2.0 / np.pi) * (v + 0.044715 * v**3)))


K, T, S, H, T3, S2, P = 1024, 4096, 1024, 512, 2048, 512, 512

def setup_inputs():
    n = np.random.standard_normal
    s = mx_kscale(K)[:, None]
    u = mx_kscale(H)[:, None]
    d = {}
    d["tab_words"], d["tab_scales"] = pack_weight(n((K, T)) * s, "e4m3")
    d["tab2_words"], d["tab2_scales"] = pack_weight(n((H, T3)) / u / H**0.5, "e4m3")
    d["offs"] = striped(np.random.permutation(T)[:S])
    d["offs2"] = striped(np.random.permutation(T3)[:S2])
    d["pos1"] = striped(np.random.permutation(S)[:P])
    d["pos2"] = striped(np.random.permutation(S)[:P])
    d["w1"] = (0.8 * n((K, H)) / s * u.T / K**0.5).astype(np.float32)
    d["w4_words"], d["w4_scales"] = pack_weight(0.8 * n((K, S2)) / s / K**0.5, "e2m1")
    d["going"] = np.exp(0.5 * n((H, S))).astype(np.float32)
    d["base"] = (0.8 * n(S2)).astype(np.float32)
    return d

def reference(tab_words, tab_scales, tab2_words, tab2_scales, offs, offs2, pos1, pos2,
              w1, w4_words, w4_scales, going, base):
    v = unpack_weight(tab_words, tab_scales, "e4m3")[:, unstriped(offs)]
    v2 = unpack_weight(tab2_words, tab2_scales, "e4m3")[:, unstriped(offs2)]
    w4 = unpack_weight(w4_words, w4_scales, "e2m1")
    h = (mxq(f64(w1), 0, "e4m3").T @ v) * f64(going)
    hq = mxq(h, 0, "e4m3")
    e = v2.T @ hq + w4.T @ v
    lead = e[:, unstriped(pos1)] - e[:, unstriped(pos2)] + f64(base)[:, None]
    return np.log(1.0 + np.exp(lead))

@@ -1,0 +1,259 @@
+from contextlib import ExitStack
+
+import concourse.mybir as mybir
+
+K, T, S, H, T3, S2, NP = 1024, 4096, 1024, 512, 2048, 512, 512
+FLOPS = 2 * K * H * S + 2 * H * S2 * S + 2 * K * S2 * S
+
+F32 = mybir.dt.float32
+BF16 = mybir.dt.bfloat16
+I32 = mybir.dt.int32
+U32 = mybir.dt.uint32
+U16 = mybir.dt.uint16
+U8 = mybir.dt.uint8
+FP8X4 = mybir.dt.float8_e4m3fn_x4
+FP4X4 = mybir.dt.float4_e2m1fn_x4
+ALU = mybir.AluOpType
+ACT = mybir.ActivationFunctionType
+
+P = 128
+PACK = 4
+PASSES = K // (P * PACK)
+CHUNK = 128
+N_CHUNKS = S // CHUNK
+HALF = 512
+GO_COLS = 256
+M_TILES = S2 // P
+CAP = 32.0
+E_BANKS = 5
+H_BANKS = 3
+CAST_SPLIT = 88
+
+
+def tile_list_handicap_rival_margin_kernel(
+    tc, tab_words, tab_scales, tab2_words, tab2_scales, offs, offs2, pos1, pos2,
+    w1, w4_words, w4_scales, going, base, out,
+):
+    nc = tc.nc
+    with ExitStack() as ctx:
+        keep = ctx.enter_context(tc.tile_pool(name="keep", bufs=1))
+        ring = ctx.enter_context(tc.tile_pool(name="ring", bufs=3))
+        psum_e = ctx.enter_context(tc.psum_pool(name="psum_e", bufs=E_BANKS))
+        psum_h = ctx.enter_context(tc.psum_pool(name="psum_h", bufs=H_BANKS))
+
+        def held(shape, dtype, name):
+            return keep.tile(shape, dtype, name=name, align_bytes=64)
+
+        offs_sb = held([P, S // 16], U16, "offs_sb")
+        offs2_sb = held([P, S2 // 16], U16, "offs2_sb")
+        pos1_sb = held([P, NP // 16], U16, "pos1_sb")
+        pos2_sb = held([P, NP // 16], U16, "pos2_sb")
+        tab_w = [held([P, T], U32, "tab_w%d" % a) for a in range(PASSES)]
+        tab_s = held([P, T], U8, "tab_s")
+        tab2_w = held([P, T3], U32, "tab2_w")
+        tab2_s = held([P, T3], U8, "tab2_s")
+        w4_w = held([P, PASSES, 2 * S2], U8, "w4_w")
+        w4_s = held([P, PASSES, S2], U8, "w4_s")
+        w1_raw = [held([P, PACK, H], F32, "w1_raw%d" % a) for a in range(PASSES)]
+        go = [held([P, PACK, GO_COLS], F32, "go%d" % i) for i in range(S // GO_COLS)]
+        base_sb = held([P, M_TILES], F32, "base_sb")
+        v_w = [held([P, S], U32, "v_w%d" % a) for a in range(PASSES)]
+        v_s = held([P, S], U8, "v_s")
+        v_s1 = held([P, S], U8, "v_s1")
+        v2_w = held([P, S2], U32, "v2_w")
+        v2_s = held([P, S2], U8, "v2_s")
+
+        nc.vector.memset(tab_s[:].bitcast(I32), 0)
+        nc.vector.memset(tab2_s[:].bitcast(I32), 0)
+        nc.vector.memset(w4_s[:].rearrange("p a c -> p (a c)").bitcast(I32), 0)
+        nc.vector.memset(v_s1[:].bitcast(I32), 0)
+        one = held([P, 1], F32, "one")
+        cap = held([P, 1], F32, "cap")
+        nc.vector.memset(one[:], 1.0)
+        nc.scalar.activation(cap[:], one[:], ACT.Copy, scale=CAP)
+
+        def words(src):
+            return src.rearrange("p t i -> p (t i)").bitcast(I32)
+
+        def load_going(i):
+            rows = going.rearrange("(p t) n -> p t n", t=PACK)
+            nc.sync.dma_start(out=go[i][:], in_=rows[:, :, i * GO_COLS : (i + 1) * GO_COLS])
+
+        nc.sync.dma_start(offs_sb[:], offs)
+        nc.sync.dma_start(offs2_sb[:], offs2)
+        nc.sync.dma_start(out=tab_w[0][:].bitcast(I32), in_=words(tab_words[0]))
+        nc.sync.dma_start(out=tab_w[1][:].bitcast(I32), in_=words(tab_words[1]))
+        for a in range(PASSES):
+            rows = w1[a * P * PACK : (a + 1) * P * PACK, :]
+            nc.sync.dma_start(out=w1_raw[a][:], in_=rows.rearrange("(p j) c -> p j c", j=PACK))
+        load_going(0)
+        load_going(1)
+        nc.sync.dma_start(out=w4_w[:].bitcast(I32), in_=w4_words.rearrange("a p c -> p a c").bitcast(I32))
+        for q in range(4):
+            nc.sync.dma_start(
+                out=w4_s[32 * q : 32 * q + 4, :, :].bitcast(I32),
+                in_=w4_scales[:, 4 * q : 4 * q + 4, :].rearrange("a r c -> r a c").bitcast(I32),
+            )
+        load_going(2)
+        nc.sync.dma_start(out=tab2_w[:].bitcast(I32), in_=words(tab2_words[0]))
+        load_going(3)
+        nc.sync.dma_start(pos2_sb[:], pos2)
+        nc.sync.dma_start(pos1_sb[:], pos1)
+        with nc.allow_non_contiguous_dma(reason="one base value for each partition and row tile"):
+            nc.sync.dma_start(out=base_sb[:], in_=base.rearrange("(m p) -> p m", p=P))
+        for q in range(4):
+            nc.gpsimd.dma_start(
+                out=tab_s[32 * q : 32 * q + 4 * PASSES, :].bitcast(I32),
+                in_=tab_scales[:, 4 * q : 4 * q + 4, :].bitcast(I32),
+            )
+        for q in range(4):
+            nc.gpsimd.dma_start(
+                out=tab2_s[32 * q : 32 * q + 4, :].bitcast(I32),
+                in_=tab2_scales[0, 4 * q : 4 * q + 4, :].bitcast(I32),
+            )
+
+        nc.vector.tensor_copy(v_w[0][:], tab_w[0][:].indirect(offs_sb[:]))
+        nc.vector.tensor_copy(v_s[:], tab_s[:].indirect(offs_sb[:]))
+        for q in range(4):
+            nc.gpsimd.dma_start(
+                out=v_s1[32 * q : 32 * q + 4, :].bitcast(I32),
+                in_=v_s[32 * q + 4 : 32 * q + 8, :].bitcast(I32),
+            )
+        nc.vector.tensor_copy(v_w[1][:], tab_w[1][:].indirect(offs_sb[:]))
+        nc.vector.tensor_copy(v2_s[:], tab2_s[:].indirect(offs2_sb[:]))
+
+        e_ps = {}
+
+        def residual_pass(m, half, a):
+            cols = slice(half * HALF, (half + 1) * HALF)
+            plane = v_s if a == 0 else v_s1
+            nc.tensor.matmul_mx(
+                out=e_ps[m, half][:],
+                lhsT=w4_w[:, a, 2 * P * m : 2 * P * (m + 1)].bitcast(FP4X4),
+                lhsT_scale=w4_s[:, a, P * m : P * (m + 1)],
+                rhs=v_w[a][:, cols].bitcast(FP8X4),
+                rhs_scale=plane[:, cols],
+                start=(a == 0),
+                stop=False,
+            )
+
+        def open_groups(groups):
+            for m, half in groups:
+                e_ps[m, half] = psum_e.tile([P, HALF], F32, name="e_ps")
+            for a in range(PASSES):
+                for m, half in groups:
+                    residual_pass(m, half, a)
+
+        groups = [(m, half) for half in range(S // HALF) for m in range(M_TILES)]
+
+        w1_w = held([P, PASSES, H], U32, "w1_w")
+        w1_s = held([P, PASSES, H], U8, "w1_s")
+        for a in range(PASSES):
+            w1_bf = held([P, PACK, P, PACK], BF16, "w1_bf%d" % a)
+            dst = w1_bf[:].rearrange("p t m j -> p m t j")
+            src = w1_raw[a][:].rearrange("p j (m t) -> p m t j", t=PACK)
+            nc.vector.tensor_copy(out=dst[:, :CAST_SPLIT], in_=src[:, :CAST_SPLIT])
+            nc.scalar.copy(out=dst[:, CAST_SPLIT:], in_=src[:, CAST_SPLIT:])
+            nc.vector.quantize_mx(
+                out=w1_w[:, a, :].bitcast(FP8X4),
+                scales=w1_s[:, a, :],
+                in_=w1_bf[:].rearrange("p t m j -> p (t m j)"),
+            )
+
+        h_w = [held([P, HALF], U32, "h_w%d" % i) for i in range(S // HALF)]
+        h_s = [held([P, HALF], U8, "h_s%d" % i) for i in range(S // HALF)]
+        e_sb = [held([P, S], F32, "e_sb%d" % m) for m in range(M_TILES)]
+        h_bf = {}
+
+        def make_h(c):
+            cols = slice(c * CHUNK, (c + 1) * CHUNK)
+            h_ps = psum_h.tile([P, PACK, CHUNK], F32, name="h_ps")
+            for a in range(PASSES):
+                for t in range(PACK):
+                    nc.tensor.matmul_mx(
+                        out=h_ps[:, t, :],
+                        lhsT=w1_w[:, a, t * P : (t + 1) * P].bitcast(FP8X4),
+                        lhsT_scale=w1_s[:, a, t * P : (t + 1) * P],
+                        rhs=v_w[a][:, cols].bitcast(FP8X4),
+                        rhs_scale=v_s[4 * a : P, cols],
+                        start=(a == 0 and t == 0),
+                        stop=(a == PASSES - 1 and t == PACK - 1),
+                    )
+            h_bf[c] = ring.tile([P, CHUNK * PACK], BF16, name="h_bf", align_bytes=64)
+            i, n0 = divmod(c * CHUNK, GO_COLS)
+            nc.vector.tensor_tensor(
+                h_bf[c][:].rearrange("p (c i t) -> p c t i", i=4, t=PACK),
+                h_ps[:].rearrange("p t (c i) -> p c t i", i=4),
+                go[i][:, :, n0 : n0 + CHUNK].rearrange("p t (c i) -> p c t i", i=4),
+                ALU.mult,
+            )
+
+        def quantize_h(c):
+            half, n0 = divmod(c * CHUNK, HALF)
+            nc.vector.quantize_mx(
+                out=h_w[half][:, n0 : n0 + CHUNK].bitcast(FP8X4),
+                scales=h_s[half][:, n0 : n0 + CHUNK],
+                in_=h_bf[c][:],
+            )
+
+        def close_group(m, half):
+            nc.tensor.matmul_mx(
+                out=e_ps[m, half][:],
+                lhsT=v2_w[:, P * m : P * (m + 1)].bitcast(FP8X4),
+                lhsT_scale=v2_s[:, P * m : P * (m + 1)],
+                rhs=h_w[half][:].bitcast(FP8X4),
+                rhs_scale=h_s[half][:],
+                start=False,
+                stop=True,
+            )
+            nc.scalar.copy(e_sb[m][:, half * HALF : (half + 1) * HALF], e_ps[m, half][:])
+
+        per_half = HALF // CHUNK
+        for c in range(N_CHUNKS):
+            make_h(c)
+            if c > 0:
+                quantize_h(c - 1)
+            if c == H_BANKS - 1:
+                open_groups(groups[:E_BANKS])
+            if c == per_half:
+                nc.vector.tensor_copy(v2_w[:], tab2_w[:].indirect(offs2_sb[:]))
+                for m in range(M_TILES):
+                    close_group(m, 0)
+        quantize_h(N_CHUNKS - 1)
+        for g in groups[E_BANKS:]:
+            open_groups([g])
+        for m in range(M_TILES):
+            close_group(m, 1)
+
+        cap_less_base = held([P, M_TILES], F32, "cap_less_base")
+        nc.scalar.activation(cap_less_base[:], base_sb[:], ACT.Identity, bias=cap[:], scale=-1.0)
+        logs = held([P, M_TILES, NP], F32, "logs")
+        room = logs[:, :, 0 : NP // M_TILES]
+        diff = [held([P, NP], F32, "diff%d" % m) for m in range(M_TILES)]
+        expo = [held([P, NP], F32, "expo%d" % m) for m in range(M_TILES)]
+        rival = {}
+
+        def pick_rival(m):
+            rival[m] = ring.tile([P, NP], F32, name="rival")
+            nc.vector.tensor_copy(rival[m][:], e_sb[m][:].indirect(pos2_sb[:]))
+
+        pick_rival(0)
+        for m in range(M_TILES):
+            if m + 1 < M_TILES:
+                pick_rival(m + 1)
+            nc.vector.tensor_tensor(diff[m][:], e_sb[m][:].indirect(pos1_sb[:]), rival[m][:], ALU.subtract)
+            nc.scalar.activation(
+                room, diff[m][:].rearrange("p (k c) -> p k c", k=M_TILES), ACT.Relu,
+                bias=cap_less_base[:, m : m + 1], scale=-1.0,
+            )
+            nc.scalar.activation(
+                expo[m][:].rearrange("p (k c) -> p k c", k=M_TILES), room, ACT.Exp,
+                bias=cap[:], scale=-1.0,
+            )
+        for m in range(M_TILES):
+            nc.scalar.activation(logs[:, m, :], expo[m][:], ACT.Ln, bias=one[:])
+            result = held([P, NP], F32, "result%d" % m)
+            nc.vector.scalar_tensor_tensor(
+                result[:], diff[m][:], base_sb[:, m : m + 1], logs[:, m, :], ALU.add, ALU.max
+            )
+            nc.sync.dma_start(out=out[m * P : (m + 1) * P, :], in_=result[:])

@@ -37,7 +37,7 @@ def tile_list_handicap_rival_margin_kernel(
     nc = tc.nc
     with ExitStack() as ctx:
         keep = ctx.enter_context(tc.tile_pool(name="keep", bufs=1))
-        ring = ctx.enter_context(tc.tile_pool(name="ring", bufs=3))
+        ring = ctx.enter_context(tc.tile_pool(name="ring", bufs=4))
         psum_e = ctx.enter_context(tc.psum_pool(name="psum_e", bufs=E_BANKS))
         psum_h = ctx.enter_context(tc.psum_pool(name="psum_h", bufs=H_BANKS))
 
@@ -54,7 +54,10 @@ def tile_list_handicap_rival_margin_kernel(
         tab2_s = held([P, T3], U8, "tab2_s")
         w4_w = held([P, PASSES, 2 * S2], U8, "w4_w")
         w4_s = held([P, PASSES, S2], U8, "w4_s")
-        w1_raw = [held([P, PACK, H], F32, "w1_raw%d" % a) for a in range(PASSES)]
+        w1_raw = [
+            [held([P, PACK, H // (a + 1)], F32, "w1_raw%d_%d" % (a, i)) for i in range(a + 1)]
+            for a in range(PASSES)
+        ]
         go = [held([P, PACK, GO_COLS], F32, "go%d" % i) for i in range(S // GO_COLS)]
         base_sb = held([P, M_TILES], F32, "base_sb")
         v_w = [held([P, S], U32, "v_w%d" % a) for a in range(PASSES)]
@@ -63,7 +66,8 @@ def tile_list_handicap_rival_margin_kernel(
         v2_w = held([P, S2], U32, "v2_w")
         v2_s = held([P, S2], U8, "v2_s")
 
-        nc.vector.memset(tab_s[:].bitcast(I32), 0)
+        nc.vector.memset(tab_s[:, : T // 2].bitcast(I32), 0)
+        nc.gpsimd.memset(tab_s[:, T // 2 :].bitcast(I32), 0)
         nc.vector.memset(tab2_s[:].bitcast(I32), 0)
         nc.vector.memset(w4_s[:].rearrange("p a c -> p (a c)").bitcast(I32), 0)
         nc.vector.memset(v_s1[:].bitcast(I32), 0)
@@ -82,45 +86,48 @@ def tile_list_handicap_rival_margin_kernel(
         nc.sync.dma_start(offs_sb[:], offs)
         nc.sync.dma_start(offs2_sb[:], offs2)
         nc.sync.dma_start(out=tab_w[0][:].bitcast(I32), in_=words(tab_words[0]))
+        nc.sync.dma_start(pos2_sb[:], pos2)
+        nc.sync.dma_start(pos1_sb[:], pos1)
+        for q in range(4):
+            nc.sync.dma_start(
+                out=tab_s[32 * q : 32 * q + 4 * PASSES, :].bitcast(I32),
+                in_=tab_scales[:, 4 * q : 4 * q + 4, :].bitcast(I32),
+            )
         nc.sync.dma_start(out=tab_w[1][:].bitcast(I32), in_=words(tab_words[1]))
         for a in range(PASSES):
             rows = w1[a * P * PACK : (a + 1) * P * PACK, :]
-            nc.sync.dma_start(out=w1_raw[a][:], in_=rows.rearrange("(p j) c -> p j c", j=PACK))
+            rows = rows.rearrange("(p j) c -> p j c", j=PACK)
+            for i, piece in enumerate(w1_raw[a]):
+                width = H // len(w1_raw[a])
+                nc.sync.dma_start(out=piece[:], in_=rows[:, :, i * width : (i + 1) * width])
         load_going(0)
-        load_going(1)
         nc.sync.dma_start(out=w4_w[:].bitcast(I32), in_=w4_words.rearrange("a p c -> p a c").bitcast(I32))
         for q in range(4):
             nc.sync.dma_start(
                 out=w4_s[32 * q : 32 * q + 4, :, :].bitcast(I32),
                 in_=w4_scales[:, 4 * q : 4 * q + 4, :].rearrange("a r c -> r a c").bitcast(I32),
             )
-        load_going(2)
-        nc.sync.dma_start(out=tab2_w[:].bitcast(I32), in_=words(tab2_words[0]))
-        load_going(3)
-        nc.sync.dma_start(pos2_sb[:], pos2)
-        nc.sync.dma_start(pos1_sb[:], pos1)
-        with nc.allow_non_contiguous_dma(reason="one base value for each partition and row tile"):
-            nc.sync.dma_start(out=base_sb[:], in_=base.rearrange("(m p) -> p m", p=P))
-        for q in range(4):
-            nc.gpsimd.dma_start(
-                out=tab_s[32 * q : 32 * q + 4 * PASSES, :].bitcast(I32),
-                in_=tab_scales[:, 4 * q : 4 * q + 4, :].bitcast(I32),
-            )
-        for q in range(4):
-            nc.gpsimd.dma_start(
-                out=tab2_s[32 * q : 32 * q + 4, :].bitcast(I32),
-                in_=tab2_scales[0, 4 * q : 4 * q + 4, :].bitcast(I32),
-            )
+        load_going(1)
 
         nc.vector.tensor_copy(v_w[0][:], tab_w[0][:].indirect(offs_sb[:]))
         nc.vector.tensor_copy(v_s[:], tab_s[:].indirect(offs_sb[:]))
+        nc.vector.tensor_copy(v_w[1][:], tab_w[1][:].indirect(offs_sb[:]))
+
+        load_going(2)
         for q in range(4):
-            nc.gpsimd.dma_start(
+            nc.sync.dma_start(
+                out=tab2_s[32 * q : 32 * q + 4, :].bitcast(I32),
+                in_=tab2_scales[0, 4 * q : 4 * q + 4, :].bitcast(I32),
+            )
+        nc.sync.dma_start(out=tab2_w[:].bitcast(I32), in_=words(tab2_words[0]))
+        for q in range(4):
+            nc.sync.dma_start(
                 out=v_s1[32 * q : 32 * q + 4, :].bitcast(I32),
                 in_=v_s[32 * q + 4 : 32 * q + 8, :].bitcast(I32),
             )
-        nc.vector.tensor_copy(v_w[1][:], tab_w[1][:].indirect(offs_sb[:]))
-        nc.vector.tensor_copy(v2_s[:], tab2_s[:].indirect(offs2_sb[:]))
+        load_going(3)
+        with nc.allow_non_contiguous_dma(reason="one base value for each partition and row tile"):
+            nc.sync.dma_start(out=base_sb[:], in_=base.rearrange("(m p) -> p m", p=P))
 
         e_ps = {}
 
@@ -144,16 +151,20 @@ def tile_list_handicap_rival_margin_kernel(
                 for m, half in groups:
                     residual_pass(m, half, a)
 
-        groups = [(m, half) for half in range(S // HALF) for m in range(M_TILES)]
+        groups = [(m, half) for m in range(M_TILES) for half in range(S // HALF)]
 
         w1_w = held([P, PASSES, H], U32, "w1_w")
         w1_s = held([P, PASSES, H], U8, "w1_s")
         for a in range(PASSES):
             w1_bf = held([P, PACK, P, PACK], BF16, "w1_bf%d" % a)
             dst = w1_bf[:].rearrange("p t m j -> p m t j")
-            src = w1_raw[a][:].rearrange("p j (m t) -> p m t j", t=PACK)
-            nc.vector.tensor_copy(out=dst[:, :CAST_SPLIT], in_=src[:, :CAST_SPLIT])
-            nc.scalar.copy(out=dst[:, CAST_SPLIT:], in_=src[:, CAST_SPLIT:])
+            for i, piece in enumerate(w1_raw[a]):
+                src = piece[:].rearrange("p j (m t) -> p m t j", t=PACK)
+                count = P // len(w1_raw[a])
+                split = count * CAST_SPLIT // P
+                m0 = i * count
+                nc.vector.tensor_copy(out=dst[:, m0 : m0 + split], in_=src[:, :split])
+                nc.scalar.copy(out=dst[:, m0 + split : m0 + count], in_=src[:, split:])
             nc.vector.quantize_mx(
                 out=w1_w[:, a, :].bitcast(FP8X4),
                 scales=w1_s[:, a, :],
@@ -179,22 +190,29 @@ def tile_list_handicap_rival_margin_kernel(
                         start=(a == 0 and t == 0),
                         stop=(a == PASSES - 1 and t == PACK - 1),
                     )
-            h_bf[c] = ring.tile([P, CHUNK * PACK], BF16, name="h_bf", align_bytes=64)
+            if c % 2 == 0:
+                h_bf[c // 2] = ring.tile([P, 2, CHUNK * PACK], BF16, name="h_bf", align_bytes=64)
             i, n0 = divmod(c * CHUNK, GO_COLS)
             nc.vector.tensor_tensor(
-                h_bf[c][:].rearrange("p (c i t) -> p c t i", i=4, t=PACK),
+                h_bf[c // 2][:, c % 2, :].rearrange("p (c i t) -> p c t i", i=4, t=PACK),
                 h_ps[:].rearrange("p t (c i) -> p c t i", i=4),
                 go[i][:, :, n0 : n0 + CHUNK].rearrange("p t (c i) -> p c t i", i=4),
                 ALU.mult,
             )
 
-        def quantize_h(c):
+        def quantize_h(c, count):
             half, n0 = divmod(c * CHUNK, HALF)
             nc.vector.quantize_mx(
-                out=h_w[half][:, n0 : n0 + CHUNK].bitcast(FP8X4),
-                scales=h_s[half][:, n0 : n0 + CHUNK],
-                in_=h_bf[c][:],
+                out=h_w[half][:, n0 : n0 + count * CHUNK].bitcast(FP8X4),
+                scales=h_s[half][:, n0 : n0 + count * CHUNK],
+                in_=h_bf[c // 2][:, c % 2 : c % 2 + count, :].rearrange("p c n -> p (c n)"),
             )
+
+        def pick_profiles(piece):
+            cols = slice(piece * S2 // 2, (piece + 1) * S2 // 2)
+            entries = offs2_sb[:, piece * S2 // 32 : (piece + 1) * S2 // 32]
+            nc.vector.tensor_copy(v2_s[:, cols], tab2_s[:].indirect(entries))
+            nc.vector.tensor_copy(v2_w[:, cols], tab2_w[:].indirect(entries))
 
         def close_group(m, half):
             nc.tensor.matmul_mx(
@@ -208,27 +226,25 @@ def tile_list_handicap_rival_margin_kernel(
             )
             nc.scalar.copy(e_sb[m][:, half * HALF : (half + 1) * HALF], e_ps[m, half][:])
 
-        per_half = HALF // CHUNK
         for c in range(N_CHUNKS):
             make_h(c)
-            if c > 0:
-                quantize_h(c - 1)
-            if c == H_BANKS - 1:
-                open_groups(groups[:E_BANKS])
-            if c == per_half:
-                nc.vector.tensor_copy(v2_w[:], tab2_w[:].indirect(offs2_sb[:]))
-                for m in range(M_TILES):
-                    close_group(m, 0)
-        quantize_h(N_CHUNKS - 1)
-        for g in groups[E_BANKS:]:
-            open_groups([g])
-        for m in range(M_TILES):
-            close_group(m, 1)
+            if c in (2, 4, 6):
+                quantize_h(c - 2, 2)
+            if c == 5:
+                pick_profiles(0)
+            if c == N_CHUNKS - 1:
+                quantize_h(c - 1, 1)
+        quantize_h(N_CHUNKS - 1, 1)
+        pick_profiles(1)
+        open_groups(groups[:E_BANKS])
+        for i, g in enumerate(groups):
+            if i >= E_BANKS:
+                open_groups([g])
+            close_group(*g)
 
         cap_less_base = held([P, M_TILES], F32, "cap_less_base")
         nc.scalar.activation(cap_less_base[:], base_sb[:], ACT.Identity, bias=cap[:], scale=-1.0)
         logs = held([P, M_TILES, NP], F32, "logs")
-        room = logs[:, :, 0 : NP // M_TILES]
         diff = [held([P, NP], F32, "diff%d" % m) for m in range(M_TILES)]
         expo = [held([P, NP], F32, "expo%d" % m) for m in range(M_TILES)]
         rival = {}
@@ -237,23 +253,33 @@ def tile_list_handicap_rival_margin_kernel(
             rival[m] = ring.tile([P, NP], F32, name="rival")
             nc.vector.tensor_copy(rival[m][:], e_sb[m][:].indirect(pos2_sb[:]))
 
+        def pieces(m):
+            count = 2 if m == M_TILES - 1 else 1
+            return [(i * NP // count, NP // count) for i in range(count)]
+
         pick_rival(0)
         for m in range(M_TILES):
             if m + 1 < M_TILES:
                 pick_rival(m + 1)
-            nc.vector.tensor_tensor(diff[m][:], e_sb[m][:].indirect(pos1_sb[:]), rival[m][:], ALU.subtract)
-            nc.scalar.activation(
-                room, diff[m][:].rearrange("p (k c) -> p k c", k=M_TILES), ACT.Relu,
-                bias=cap_less_base[:, m : m + 1], scale=-1.0,
-            )
-            nc.scalar.activation(
-                expo[m][:].rearrange("p (k c) -> p k c", k=M_TILES), room, ACT.Exp,
-                bias=cap[:], scale=-1.0,
-            )
+            for n0, width in pieces(m):
+                cols = slice(n0, n0 + width)
+                entries = pos1_sb[:, n0 // 16 : (n0 + width) // 16]
+                nc.vector.tensor_tensor(diff[m][:, cols], e_sb[m][:].indirect(entries), rival[m][:, cols], ALU.subtract)
+                room = logs[:, :, n0 // M_TILES : (n0 + width) // M_TILES]
+                nc.scalar.activation(
+                    room, diff[m][:, cols].rearrange("p (k c) -> p k c", k=M_TILES), ACT.Relu,
+                    bias=cap_less_base[:, m : m + 1], scale=-1.0,
+                )
+                nc.scalar.activation(
+                    expo[m][:, cols].rearrange("p (k c) -> p k c", k=M_TILES), room, ACT.Exp,
+                    bias=cap[:], scale=-1.0,
+                )
         for m in range(M_TILES):
-            nc.scalar.activation(logs[:, m, :], expo[m][:], ACT.Ln, bias=one[:])
             result = held([P, NP], F32, "result%d" % m)
-            nc.vector.scalar_tensor_tensor(
-                result[:], diff[m][:], base_sb[:, m : m + 1], logs[:, m, :], ALU.add, ALU.max
-            )
-            nc.sync.dma_start(out=out[m * P : (m + 1) * P, :], in_=result[:])
+            for n0, width in pieces(m):
+                cols = slice(n0, n0 + width)
+                nc.scalar.activation(logs[:, m, cols], expo[m][:, cols], ACT.Ln, bias=one[:])
+                nc.vector.scalar_tensor_tensor(
+                    result[:, cols], diff[m][:, cols], base_sb[:, m : m + 1], logs[:, m, cols], ALU.add, ALU.max
+                )
+                nc.sync.dma_start(out=out[m * P : (m + 1) * P, cols], in_=result[:, cols])

from contextlib import ExitStack

import concourse.mybir as mybir

K, T, S, H, T3, S2, NP = 1024, 4096, 1024, 512, 2048, 512, 512
FLOPS = 2 * K * H * S + 2 * H * S2 * S + 2 * K * S2 * S

F32 = mybir.dt.float32
BF16 = mybir.dt.bfloat16
I32 = mybir.dt.int32
U32 = mybir.dt.uint32
U16 = mybir.dt.uint16
U8 = mybir.dt.uint8
FP8X4 = mybir.dt.float8_e4m3fn_x4
FP4X4 = mybir.dt.float4_e2m1fn_x4
ALU = mybir.AluOpType
ACT = mybir.ActivationFunctionType

P = 128
PACK = 4
PASSES = K // (P * PACK)
CHUNK = 128
N_CHUNKS = S // CHUNK
HALF = 512
GO_COLS = 256
M_TILES = S2 // P
CAP = 32.0
E_BANKS = 5
H_BANKS = 3
CAST_SPLIT = 88


def tile_list_handicap_rival_margin_kernel(
    tc, tab_words, tab_scales, tab2_words, tab2_scales, offs, offs2, pos1, pos2,
    w1, w4_words, w4_scales, going, base, out,
):
    nc = tc.nc
    with ExitStack() as ctx:
        keep = ctx.enter_context(tc.tile_pool(name="keep", bufs=1))
        ring = ctx.enter_context(tc.tile_pool(name="ring", bufs=4))
        psum_e = ctx.enter_context(tc.psum_pool(name="psum_e", bufs=E_BANKS))
        psum_h = ctx.enter_context(tc.psum_pool(name="psum_h", bufs=H_BANKS))

        def held(shape, dtype, name):
            return keep.tile(shape, dtype, name=name, align_bytes=64)

        offs_sb = held([P, S // 16], U16, "offs_sb")
        offs2_sb = held([P, S2 // 16], U16, "offs2_sb")
        pos1_sb = held([P, NP // 16], U16, "pos1_sb")
        pos2_sb = held([P, NP // 16], U16, "pos2_sb")
        tab_w = [held([P, T], U32, "tab_w%d" % a) for a in range(PASSES)]
        tab_s = held([P, T], U8, "tab_s")
        tab2_w = held([P, T3], U32, "tab2_w")
        tab2_s = held([P, T3], U8, "tab2_s")
        w4_w = held([P, PASSES, 2 * S2], U8, "w4_w")
        w4_s = held([P, PASSES, S2], U8, "w4_s")
        w1_raw = [
            [held([P, PACK, H // (a + 1)], F32, "w1_raw%d_%d" % (a, i)) for i in range(a + 1)]
            for a in range(PASSES)
        ]
        go = [held([P, PACK, GO_COLS], F32, "go%d" % i) for i in range(S // GO_COLS)]
        base_sb = held([P, M_TILES], F32, "base_sb")
        v_w = [held([P, S], U32, "v_w%d" % a) for a in range(PASSES)]
        v_s = held([P, S], U8, "v_s")
        v_s1 = held([P, S], U8, "v_s1")
        v2_w = held([P, S2], U32, "v2_w")
        v2_s = held([P, S2], U8, "v2_s")

        nc.vector.memset(tab_s[:, : T // 2].bitcast(I32), 0)
        nc.gpsimd.memset(tab_s[:, T // 2 :].bitcast(I32), 0)
        nc.vector.memset(tab2_s[:].bitcast(I32), 0)
        nc.vector.memset(w4_s[:].rearrange("p a c -> p (a c)").bitcast(I32), 0)
        nc.vector.memset(v_s1[:].bitcast(I32), 0)
        one = held([P, 1], F32, "one")
        cap = held([P, 1], F32, "cap")
        nc.vector.memset(one[:], 1.0)
        nc.scalar.activation(cap[:], one[:], ACT.Copy, scale=CAP)

        def words(src):
            return src.rearrange("p t i -> p (t i)").bitcast(I32)

        def load_going(i):
            rows = going.rearrange("(p t) n -> p t n", t=PACK)
            nc.sync.dma_start(out=go[i][:], in_=rows[:, :, i * GO_COLS : (i + 1) * GO_COLS])

        nc.sync.dma_start(offs_sb[:], offs)
        nc.sync.dma_start(offs2_sb[:], offs2)
        nc.sync.dma_start(out=tab_w[0][:].bitcast(I32), in_=words(tab_words[0]))
        nc.sync.dma_start(pos2_sb[:], pos2)
        nc.sync.dma_start(pos1_sb[:], pos1)
        for q in range(4):
            nc.sync.dma_start(
                out=tab_s[32 * q : 32 * q + 4 * PASSES, :].bitcast(I32),
                in_=tab_scales[:, 4 * q : 4 * q + 4, :].bitcast(I32),
            )
        nc.sync.dma_start(out=tab_w[1][:].bitcast(I32), in_=words(tab_words[1]))
        for a in range(PASSES):
            rows = w1[a * P * PACK : (a + 1) * P * PACK, :]
            rows = rows.rearrange("(p j) c -> p j c", j=PACK)
            for i, piece in enumerate(w1_raw[a]):
                width = H // len(w1_raw[a])
                nc.sync.dma_start(out=piece[:], in_=rows[:, :, i * width : (i + 1) * width])
        load_going(0)
        nc.sync.dma_start(out=w4_w[:].bitcast(I32), in_=w4_words.rearrange("a p c -> p a c").bitcast(I32))
        for q in range(4):
            nc.sync.dma_start(
                out=w4_s[32 * q : 32 * q + 4, :, :].bitcast(I32),
                in_=w4_scales[:, 4 * q : 4 * q + 4, :].rearrange("a r c -> r a c").bitcast(I32),
            )
        load_going(1)

        nc.vector.tensor_copy(v_w[0][:], tab_w[0][:].indirect(offs_sb[:]))
        nc.vector.tensor_copy(v_s[:], tab_s[:].indirect(offs_sb[:]))
        nc.vector.tensor_copy(v_w[1][:], tab_w[1][:].indirect(offs_sb[:]))

        load_going(2)
        for q in range(4):
            nc.sync.dma_start(
                out=tab2_s[32 * q : 32 * q + 4, :].bitcast(I32),
                in_=tab2_scales[0, 4 * q : 4 * q + 4, :].bitcast(I32),
            )
        nc.sync.dma_start(out=tab2_w[:].bitcast(I32), in_=words(tab2_words[0]))
        for q in range(4):
            nc.sync.dma_start(
                out=v_s1[32 * q : 32 * q + 4, :].bitcast(I32),
                in_=v_s[32 * q + 4 : 32 * q + 8, :].bitcast(I32),
            )
        load_going(3)
        with nc.allow_non_contiguous_dma(reason="one base value for each partition and row tile"):
            nc.sync.dma_start(out=base_sb[:], in_=base.rearrange("(m p) -> p m", p=P))

        e_ps = {}

        def residual_pass(m, half, a):
            cols = slice(half * HALF, (half + 1) * HALF)
            plane = v_s if a == 0 else v_s1
            nc.tensor.matmul_mx(
                out=e_ps[m, half][:],
                lhsT=w4_w[:, a, 2 * P * m : 2 * P * (m + 1)].bitcast(FP4X4),
                lhsT_scale=w4_s[:, a, P * m : P * (m + 1)],
                rhs=v_w[a][:, cols].bitcast(FP8X4),
                rhs_scale=plane[:, cols],
                start=(a == 0),
                stop=False,
            )

        def open_groups(groups):
            for m, half in groups:
                e_ps[m, half] = psum_e.tile([P, HALF], F32, name="e_ps")
            for a in range(PASSES):
                for m, half in groups:
                    residual_pass(m, half, a)

        groups = [(m, half) for m in range(M_TILES) for half in range(S // HALF)]

        w1_w = held([P, PASSES, H], U32, "w1_w")
        w1_s = held([P, PASSES, H], U8, "w1_s")
        for a in range(PASSES):
            w1_bf = held([P, PACK, P, PACK], BF16, "w1_bf%d" % a)
            dst = w1_bf[:].rearrange("p t m j -> p m t j")
            for i, piece in enumerate(w1_raw[a]):
                src = piece[:].rearrange("p j (m t) -> p m t j", t=PACK)
                count = P // len(w1_raw[a])
                split = count * CAST_SPLIT // P
                m0 = i * count
                nc.vector.tensor_copy(out=dst[:, m0 : m0 + split], in_=src[:, :split])
                nc.scalar.copy(out=dst[:, m0 + split : m0 + count], in_=src[:, split:])
            nc.vector.quantize_mx(
                out=w1_w[:, a, :].bitcast(FP8X4),
                scales=w1_s[:, a, :],
                in_=w1_bf[:].rearrange("p t m j -> p (t m j)"),
            )

        h_w = [held([P, HALF], U32, "h_w%d" % i) for i in range(S // HALF)]
        h_s = [held([P, HALF], U8, "h_s%d" % i) for i in range(S // HALF)]
        e_sb = [held([P, S], F32, "e_sb%d" % m) for m in range(M_TILES)]
        h_bf = {}

        def make_h(c):
            cols = slice(c * CHUNK, (c + 1) * CHUNK)
            h_ps = psum_h.tile([P, PACK, CHUNK], F32, name="h_ps")
            for a in range(PASSES):
                for t in range(PACK):
                    nc.tensor.matmul_mx(
                        out=h_ps[:, t, :],
                        lhsT=w1_w[:, a, t * P : (t + 1) * P].bitcast(FP8X4),
                        lhsT_scale=w1_s[:, a, t * P : (t + 1) * P],
                        rhs=v_w[a][:, cols].bitcast(FP8X4),
                        rhs_scale=v_s[4 * a : P, cols],
                        start=(a == 0 and t == 0),
                        stop=(a == PASSES - 1 and t == PACK - 1),
                    )
            if c % 2 == 0:
                h_bf[c // 2] = ring.tile([P, 2, CHUNK * PACK], BF16, name="h_bf", align_bytes=64)
            i, n0 = divmod(c * CHUNK, GO_COLS)
            nc.vector.tensor_tensor(
                h_bf[c // 2][:, c % 2, :].rearrange("p (c i t) -> p c t i", i=4, t=PACK),
                h_ps[:].rearrange("p t (c i) -> p c t i", i=4),
                go[i][:, :, n0 : n0 + CHUNK].rearrange("p t (c i) -> p c t i", i=4),
                ALU.mult,
            )

        def quantize_h(c, count):
            half, n0 = divmod(c * CHUNK, HALF)
            nc.vector.quantize_mx(
                out=h_w[half][:, n0 : n0 + count * CHUNK].bitcast(FP8X4),
                scales=h_s[half][:, n0 : n0 + count * CHUNK],
                in_=h_bf[c // 2][:, c % 2 : c % 2 + count, :].rearrange("p c n -> p (c n)"),
            )

        def pick_profiles(piece):
            cols = slice(piece * S2 // 2, (piece + 1) * S2 // 2)
            entries = offs2_sb[:, piece * S2 // 32 : (piece + 1) * S2 // 32]
            nc.vector.tensor_copy(v2_s[:, cols], tab2_s[:].indirect(entries))
            nc.vector.tensor_copy(v2_w[:, cols], tab2_w[:].indirect(entries))

        def close_group(m, half):
            nc.tensor.matmul_mx(
                out=e_ps[m, half][:],
                lhsT=v2_w[:, P * m : P * (m + 1)].bitcast(FP8X4),
                lhsT_scale=v2_s[:, P * m : P * (m + 1)],
                rhs=h_w[half][:].bitcast(FP8X4),
                rhs_scale=h_s[half][:],
                start=False,
                stop=True,
            )
            nc.scalar.copy(e_sb[m][:, half * HALF : (half + 1) * HALF], e_ps[m, half][:])

        for c in range(N_CHUNKS):
            make_h(c)
            if c in (2, 4, 6):
                quantize_h(c - 2, 2)
            if c == 5:
                pick_profiles(0)
            if c == N_CHUNKS - 1:
                quantize_h(c - 1, 1)
        quantize_h(N_CHUNKS - 1, 1)
        pick_profiles(1)
        open_groups(groups[:E_BANKS])
        for i, g in enumerate(groups):
            if i >= E_BANKS:
                open_groups([g])
            close_group(*g)

        cap_less_base = held([P, M_TILES], F32, "cap_less_base")
        nc.scalar.activation(cap_less_base[:], base_sb[:], ACT.Identity, bias=cap[:], scale=-1.0)
        logs = held([P, M_TILES, NP], F32, "logs")
        diff = [held([P, NP], F32, "diff%d" % m) for m in range(M_TILES)]
        expo = [held([P, NP], F32, "expo%d" % m) for m in range(M_TILES)]
        rival = {}

        def pick_rival(m):
            rival[m] = ring.tile([P, NP], F32, name="rival")
            nc.vector.tensor_copy(rival[m][:], e_sb[m][:].indirect(pos2_sb[:]))

        def pieces(m):
            count = 2 if m == M_TILES - 1 else 1
            return [(i * NP // count, NP // count) for i in range(count)]

        pick_rival(0)
        for m in range(M_TILES):
            if m + 1 < M_TILES:
                pick_rival(m + 1)
            for n0, width in pieces(m):
                cols = slice(n0, n0 + width)
                entries = pos1_sb[:, n0 // 16 : (n0 + width) // 16]
                nc.vector.tensor_tensor(diff[m][:, cols], e_sb[m][:].indirect(entries), rival[m][:, cols], ALU.subtract)
                room = logs[:, :, n0 // M_TILES : (n0 + width) // M_TILES]
                nc.scalar.activation(
                    room, diff[m][:, cols].rearrange("p (k c) -> p k c", k=M_TILES), ACT.Relu,
                    bias=cap_less_base[:, m : m + 1], scale=-1.0,
                )
                nc.scalar.activation(
                    expo[m][:, cols].rearrange("p (k c) -> p k c", k=M_TILES), room, ACT.Exp,
                    bias=cap[:], scale=-1.0,
                )
        for m in range(M_TILES):
            result = held([P, NP], F32, "result%d" % m)
            for n0, width in pieces(m):
                cols = slice(n0, n0 + width)
                nc.scalar.activation(logs[:, m, cols], expo[m][:, cols], ACT.Ln, bias=one[:])
                nc.vector.scalar_tensor_tensor(
                    result[:, cols], diff[m][:, cols], base_sb[:, m : m + 1], logs[:, m, cols], ALU.add, ALU.max
                )
                nc.sync.dma_start(out=out[m * P : (m + 1) * P, cols], in_=result[:, cols])
